import numpy as np
import ml_dtypes


def mxq(x, axis, fmt="e4m3"):
    dtype, down = {"e4m3": (ml_dtypes.float8_e4m3fn, 7), "e5m2": (ml_dtypes.float8_e5m2, 14)}[fmt]
    v = np.moveaxis(np.asarray(x, np.float32).astype(ml_dtypes.bfloat16).astype(np.float64), axis, -1)
    blocks = v.reshape(v.shape[:-1] + (-1, 32))
    amax = np.abs(blocks).max(-1, keepdims=True)
    byte = np.maximum(np.where(amax > 0, np.frexp(amax)[1] - 1 + 127, 0) - down, 1)
    scale = np.exp2(byte - 127.0)
    codes = (blocks / scale).astype(np.float32).astype(dtype).astype(np.float64)
    return np.moveaxis((codes * scale).reshape(v.shape), -1, axis)


WIDE = False


def mx_kscale(k):
    if not WIDE:
        return np.ones(k)
    levels = np.array([10, -10, 5, -5, 0])
    if k % 512:
        return np.exp2(np.random.permutation(np.resize(levels, k // 32))).repeat(32)
    a = np.empty((k // 512, 16))
    for p in range(k // 512):
        a[p, :8] = np.random.permutation(np.resize(levels, 8))
        for g in range(8):
            far = levels[np.abs(levels - a[p, g]) >= 10]
            a[p, g + 8] = far[np.random.randint(len(far))]
    return np.exp2(a.ravel()).repeat(32)


BF16 = ml_dtypes.bfloat16


def bf(x):
    return np.asarray(x, np.float32).astype(BF16)


def f64(x):
    return np.asarray(x).astype(np.float64)


E2M1 = np.array([0.0, 0.5, 1.0, 1.5, 2.0, 3.0, 4.0, 6.0, -0.0, -0.5, -1.0, -1.5, -2.0, -3.0, -4.0, -6.0])


def pack_weight(w, fmt):
    k, n = w.shape
    w = f64(bf(w)).reshape(k // 32, 32, n)
    amax = np.abs(w).max(1)
    if fmt == "e4m3":
        byte = np.frexp(amax)[1] - 1 + 127 - 7
    else:
        mant, ex = np.frexp(amax / 6.0)
        byte = np.where(mant > 0.5, ex, ex - 1) + 127
    byte = np.clip(np.where(amax > 0, byte, 1), 1, 254)
    scaled = (w * np.exp2(127.0 - byte)[:, None, :]).reshape(k, n).astype(np.float32)
    by_word = np.ascontiguousarray(scaled.reshape(k // 512, 128, 4, n).transpose(0, 1, 3, 2))
    if fmt == "e4m3":
        words = by_word.astype(ml_dtypes.float8_e4m3fn).view(np.uint8)
    else:
        c = by_word.astype(ml_dtypes.float4_e2m1fn).view(np.uint8) & 0xF
        words = c[..., 0::2] | (c[..., 1::2] << 4)
    return np.ascontiguousarray(words), np.ascontiguousarray(byte.astype(np.uint8).reshape(k // 512, 16, n))


def unpack_weight(words, scales, fmt):
    g, p, n, _ = words.shape
    if fmt == "e4m3":
        vals = np.ascontiguousarray(words).view(ml_dtypes.float8_e4m3fn).astype(np.float64)
    else:
        nib = np.empty((g, p, n, 4), np.uint8)
        nib[..., 0::2] = words & 0xF
        nib[..., 1::2] = words >> 4
        vals = E2M1[nib]
    vals = vals * np.repeat(np.exp2(scales.astype(np.float64) - 127.0), 8, axis=1)[..., None]
    return vals.transpose(0, 1, 3, 2).reshape(g * 512, n)
def pack4(w):
    words, scales = pack_weight(w, "e2m1")
    return words.reshape(words.shape[0], 128, -1), scales


def unpack4(words, scales):
    return unpack_weight(words.reshape(words.shape[0], 128, -1, 2), scales, "e2m1")


def planes(Y):
    n, m = Y.shape
    b = f64(bf(Y)).reshape(n // 32, 32, m)
    amax = np.abs(b).max(1)
    byte = np.clip(np.where(amax > 0, np.frexp(amax)[1] - 1 + 127 - 7, 1), 1, 254)
    codes = (b * np.exp2(127.0 - byte)[:, None, :]).reshape(n, m).astype(np.float32).astype(ml_dtypes.float8_e4m3fn).view(np.uint8)
    words = codes.reshape(n // 512, 128, 4, m).transpose(0, 1, 3, 2)
    return np.ascontiguousarray(words), np.ascontiguousarray(byte.astype(np.uint8).reshape(n // 512, 16, m))


B, N, E = 768, 2048, 1024

SPREAD_ROWS, SPREAD_LAM, SPREAD_SIG = 0.5, 0.9, 0.7
SHIFT, FLOOR = 0.4, 0.5


def setup_inputs():
    rn = np.random.randn
    s, t = mx_kscale(N), mx_kscale(E)
    V = np.linalg.qr(np.exp(SPREAD_ROWS * rn(N, 1)) * rn(N, E))[0]
    lam = np.exp(SPREAD_LAM * rn(E)) - SHIFT
    floor = FLOOR * np.exp(0.2 * rn(E))
    r = 1.0 / np.sqrt((V * V * np.maximum(lam, floor)).sum(axis=1))
    X = rn(N, B)
    P = r[:, None] * V
    sig = np.exp(SPREAD_SIG * rn(N))
    mu = 0.5 * sig * rn(N)
    x_words, x_scales = pack4(X * s[:, None])
    p_words, p_scales = pack4(P / s[:, None])
    return {"x_words": x_words, "x_scales": x_scales, "p_words": p_words, "p_scales": p_scales,
            "vt": bf(V.T / t[:, None]), "lam": bf(lam * t), "floor": bf(floor * t),
            "r": bf(r), "sig": bf(sig), "mu": bf(mu)}

def reference(x_words, x_scales, p_words, p_scales, vt, lam, floor, r, sig, mu):
    X = unpack4(x_words, x_scales)
    P = unpack4(p_words, p_scales)
    Z = X.T @ P
    H = np.maximum(f64(lam), f64(floor)) * Z
    G = mxq(H, 1, "e4m3") @ mxq(f64(vt), 0, "e4m3")
    y = f64(sig) * (f64(r) * G) - f64(mu)
    Y = y.T
    words, scales = planes(Y)
    return y, words, scales

@@ -1,0 +1,358 @@
+from contextlib import ExitStack
+
+import concourse.mybir as mybir
+from concourse.masks import make_identity
+
+B, N, E = 768, 2048, 1024
+FLOPS = 2 * B * N * E * 2
+
+F32 = mybir.dt.float32
+BF16 = mybir.dt.bfloat16
+I32 = mybir.dt.int32
+U32 = mybir.dt.uint32
+U8 = mybir.dt.uint8
+FP8X4 = mybir.dt.float8_e4m3fn_x4
+FP4X4 = mybir.dt.float4_e2m1fn_x4
+ACT = mybir.ActivationFunctionType
+ALU = mybir.AluOpType
+
+P = 128
+WIDE = slice(0, 512)
+NARROW = slice(512, 768)
+
+
+def tile_clipped_correlation_risk_gradient_k5_kernel(
+    tc, x_words, x_scales, p_words, p_scales, vt, lam, floor, r, sig, mu, out_0, out_1, out_2
+):
+    nc = tc.nc
+    with ExitStack() as ctx:
+        keep = ctx.enter_context(tc.tile_pool(name="keep", bufs=1))
+        ring = ctx.enter_context(tc.tile_pool(name="ring", bufs=2))
+        psum = ctx.enter_context(tc.psum_pool(name="psum", bufs=8))
+        ctx.enter_context(tc.manual_schedule())
+
+        x_codes = keep.tile([P, 4, 2 * B], U8, align_bytes=64)
+        x_plane = keep.tile([P, 4, B], U8, align_bytes=64)
+        p_raw = keep.tile([P, 4, 2 * E], U8, align_bytes=64)
+        p_raw_plane = keep.tile([P, 4, E], U8, align_bytes=64)
+        p_codes = keep.tile([P, 4, 8, 2 * P], U8, align_bytes=64)
+        p_plane = keep.tile([P, 4, 8, P], U8, align_bytes=64)
+        vt_raw = keep.tile([P, 2, 4, N], BF16, align_bytes=64)
+        vt_codes = keep.tile([P, 4, 2, 512], U32, align_bytes=64)
+        vt_plane = keep.tile([P, 4, 2, 512], U8, align_bytes=64)
+        h_rows = keep.tile([P, 2, 4, B], BF16, align_bytes=64)
+        h_grouped = keep.tile([P, 2, B, 4], BF16, align_bytes=64)
+        h_codes = keep.tile([P, 2, B], U32, align_bytes=64)
+        h_plane = keep.tile([P, 2, B], U8, align_bytes=64)
+        y_codes = keep.tile([P, 4, B], U32, align_bytes=64)
+        y_plane = keep.tile([P, 4, B], U8, align_bytes=64)
+        ident = keep.tile([P, P], F32, align_bytes=64)
+        vec_rows = keep.tile([P, 512], BF16, align_bytes=64)
+        vec_f32 = keep.tile([P, 4, P], F32, align_bytes=64)
+        vec_cols = keep.tile([P, 4, 36], F32, align_bytes=64)
+        gain = keep.tile([P, 4, 4], F32, align_bytes=64)
+        neg_mu = keep.tile([P, 4, 4], F32, align_bytes=64)
+        lam_floored = keep.tile([P, 4, 2], F32, align_bytes=64)
+
+        vt_grouped = {}
+        y_t = {}
+        y_grouped = {}
+        y_rows = {}
+        banks = {}
+
+        def new_bank(key):
+            banks[key] = psum.tile([P, 512], F32, name="bank")
+            return banks[key]
+
+        def load_words(dst, src, lo, hi):
+            nc.sync.dma_start(
+                out=dst[:].bitcast(I32)[:, :, lo:hi],
+                in_=src.bitcast(I32).rearrange("g p w -> p g w")[:, :, lo:hi],
+            )
+
+        def load_scale_rows(eng, dst, src, quad):
+            eng.dma_start(
+                out=dst[:].bitcast(I32)[32 * quad : 32 * quad + 4, :, :],
+                in_=src.bitcast(I32)[:, 4 * quad : 4 * quad + 4, :].rearrange("g r w -> r g w"),
+            )
+
+        def load_vt(half, lo, hi):
+            rows = vt[512 * half : 512 * (half + 1), lo:hi].rearrange("(q t b) n -> b q t n", t=4, b=4)
+            for b in range(4):
+                nc.sync.dma_start(out=vt_raw[b:P:4, half, :, lo:hi], in_=rows[b])
+
+        def permute_p(half, t0, t1):
+            tiles = slice(4 * half + t0, 4 * half + t1)
+            words = p_raw[:].bitcast(I32).rearrange("p k (h q t w) -> p k h t q w", h=2, t=4, w=2)
+            nc.vector.tensor_copy(
+                out=p_codes[:].bitcast(I32)[:, :, tiles, :].rearrange("p k t (q w) -> p k t q w", w=2),
+                in_=words[:, :, half, t0:t1, :, :],
+            )
+            quads = p_raw_plane[:].bitcast(I32).rearrange("p k (h q t) -> p k h t q", h=2, t=4)
+            nc.vector.tensor_copy(out=p_plane[:].bitcast(I32)[:, :, tiles, :], in_=quads[:, :, half, t0:t1, :])
+
+        def stage1(acc, half, t, cols):
+            for k in range(4):
+                nc.tensor.matmul_mx(
+                    out=acc,
+                    lhsT=p_codes[:, k, 4 * half + t, :].bitcast(FP4X4),
+                    lhsT_scale=p_plane[:, k, 4 * half + t, :],
+                    rhs=x_codes[:, k, 2 * cols.start : 2 * cols.stop].bitcast(FP4X4),
+                    rhs_scale=x_plane[:, k, cols],
+                    start=(k == 0),
+                    stop=(k == 3),
+                )
+
+        def evac_h(acc, half, t, cols):
+            nc.scalar.activation(
+                out=h_rows[:, half, t, cols], in_=acc, func=ACT.Copy, scale=lam_floored[:, t, half : half + 1]
+            )
+
+        def interleave(dst, src):
+            nc.vector.tensor_copy(
+                out=dst.rearrange("p (c i) t -> p c t i", i=4), in_=src.rearrange("p t (c i) -> p c t i", i=4)
+            )
+
+        def quantize(codes, plane, grouped):
+            nc.vector.quantize_mx(out=codes.bitcast(FP8X4), scales=plane, in_=grouped)
+
+        def group_h(half, cols):
+            interleave(h_grouped[:, half, cols, :], h_rows[:, half, :, cols])
+
+        def quantize_h(half, cols):
+            quantize(
+                h_codes[:, half, cols],
+                h_plane[:, half, cols],
+                h_grouped[:, half, cols, :].rearrange("p b t -> p (b t)"),
+            )
+
+        def group_vt(g, half, on_scalar=False, part=None):
+            if (g, half) not in vt_grouped:
+                vt_grouped[(g, half)] = ring.tile([P, 2048], BF16, name="vt_grouped", bufs=4, align_bytes=64)
+            dst = vt_grouped[(g, half)][:].rearrange("p (t a m j) -> p a t j m", t=4, m=2, j=4)
+            src = vt_raw[:, half, :, 512 * g : 512 * (g + 1)].rearrange("p j (a m t) -> p a t j m", m=2, t=4)
+            if part is not None:
+                dst = dst[:, 32 * part : 32 * (part + 1)]
+                src = src[:, 32 * part : 32 * (part + 1)]
+            if on_scalar:
+                nc.scalar.copy(out=dst, in_=src)
+            else:
+                nc.vector.tensor_copy(out=dst, in_=src)
+
+        def quantize_vt(g, half):
+            quantize(vt_codes[:, g, half, :], vt_plane[:, g, half, :], vt_grouped[(g, half)][:])
+
+        def stage2(acc, g, t, cols):
+            for half in range(2):
+                nc.tensor.matmul_mx(
+                    out=acc,
+                    lhsT=vt_codes[:, g, half, P * t : P * (t + 1)].bitcast(FP8X4),
+                    lhsT_scale=vt_plane[:, g, half, P * t : P * (t + 1)],
+                    rhs=h_codes[:, half, cols].bitcast(FP8X4),
+                    rhs_scale=h_plane[:, half, cols],
+                    start=(half == 0),
+                    stop=(half == 1),
+                )
+
+        def evac_y(acc, g, t, cols, on_scalar=True):
+            if on_scalar:
+                nc.scalar.activation(
+                    out=y_t[g][:, t, cols],
+                    in_=acc,
+                    func=ACT.Identity,
+                    scale=gain[:, t, g : g + 1],
+                    bias=neg_mu[:, t, g : g + 1],
+                )
+            else:
+                nc.vector.tensor_scalar(
+                    out=y_t[g][:, t, cols],
+                    in0=acc,
+                    scalar1=gain[:, t, g : g + 1],
+                    scalar2=neg_mu[:, t, g : g + 1],
+                    op0=ALU.mult,
+                    op1=ALU.add,
+                )
+
+        def group_y(g, cols):
+            if g not in y_grouped:
+                y_grouped[g] = ring.tile([P, B, 4], BF16, name="y_grouped", align_bytes=64)
+            interleave(y_grouped[g][:, cols, :], y_t[g][:, :, cols])
+
+        def quantize_y(g, cols):
+            quantize(
+                y_codes[:, g, cols], y_plane[:, g, cols], y_grouped[g][:, cols, :].rearrange("p b t -> p (b t)")
+            )
+
+        def turn_y(g, j):
+            bank = new_bank(("turn", g, j))
+            for t in range(4):
+                nc.tensor.transpose(bank[:, P * t : P * (t + 1)], y_t[g][:, t, P * j : P * (j + 1)], ident[:])
+
+        def evac_turned(g, j, on_scalar):
+            dst = y_rows[g][:, j, :].rearrange("p (m t) -> p m t", t=4)
+            src = banks[("turn", g, j)][:].rearrange("p (t m) -> p m t", t=4)
+            if on_scalar:
+                nc.scalar.copy(out=dst, in_=src)
+            else:
+                nc.vector.tensor_copy(out=dst, in_=src)
+
+        def store_y(g, j0, j1):
+            nc.sync.dma_start(
+                out=out_0[P * j0 : P * j1, 512 * g : 512 * (g + 1)].rearrange("(j p) n -> p j n", p=P),
+                in_=y_rows[g][:, j0:j1, :],
+            )
+
+        def store_codes(g):
+            nc.sync.dma_start(
+                out=out_1[g].rearrange("p m t -> p (m t)").bitcast(I32), in_=y_codes[:, g, :].bitcast(I32)
+            )
+
+        def store_scales(g0, g1):
+            for quad in range(4):
+                nc.sync.dma_start(
+                    out=out_2.bitcast(I32)[g0:g1, 4 * quad : 4 * quad + 4, :].rearrange("g r w -> r g w"),
+                    in_=y_plane[:].bitcast(I32)[32 * quad : 32 * quad + 4, g0:g1, :],
+                )
+
+        nc.vector.memset(p_raw_plane[:].bitcast(I32), 0)
+        nc.vector.memset(x_plane[:].bitcast(I32), 0)
+        nc.vector.memset(vec_f32[:, 0, :], 0.0)
+        load_words(p_raw, p_words, 0, 256)
+        load_words(x_codes, x_words, 0, 256)
+        for quad in range(4):
+            load_scale_rows(nc.sync, p_raw_plane, p_scales, quad)
+        for quad in range(2):
+            load_scale_rows(nc.sync, x_plane, x_scales, quad)
+        for row, vec in ((32, lam), (34, floor)):
+            nc.gpsimd.dma_start(out=vec_rows[row : row + 2, :], in_=vec.rearrange("(h c) -> h c", c=512))
+        for quad in range(2, 4):
+            load_scale_rows(nc.gpsimd, x_plane, x_scales, quad)
+        make_identity(nc, ident[:])
+        for row, vec in ((0, r), (4, sig), (8, mu)):
+            nc.gpsimd.dma_start(out=vec_rows[row : row + 4, :], in_=vec.rearrange("(g c) -> g c", c=512))
+        load_vt(0, 0, 512)
+        load_words(p_raw, p_words, 256, 512)
+        load_vt(1, 0, 512)
+        load_vt(0, 512, 1024)
+        load_vt(1, 512, 1024)
+        load_words(x_codes, x_words, 256, 384)
+        load_vt(0, 1024, 2048)
+        load_vt(1, 1024, 2048)
+
+        def turn_vectors(key, lo, hi):
+            bank = new_bank(key)
+            for t in range(4):
+                nc.tensor.transpose(bank[:, P * t : P * (t + 1)], vec_f32[:, t, :], ident[:])
+            nc.scalar.copy(
+                out=vec_cols[:, :, lo:hi], in_=bank[:].rearrange("p (t v) -> p t v", t=4)[:, :, lo:hi]
+            )
+
+        for t in range(1, 4):
+            nc.scalar.activation(out=vec_f32[:, t, :], in_=vec_f32[:, 0, :], func=ACT.Copy)
+        nc.scalar.activation(
+            out=vec_f32[32:36, :, :].rearrange("v t (q b) -> v t q b", b=4),
+            in_=vec_rows[32:36, :].rearrange("v (q t b) -> v t q b", t=4, b=4),
+            func=ACT.Copy,
+        )
+        turn_vectors("vec_e", 32, 36)
+        permute_p(0, 0, 1)
+        permute_p(0, 1, 4)
+        nc.vector.tensor_tensor(
+            out=lam_floored[:], in0=vec_cols[:, :, 32:34], in1=vec_cols[:, :, 34:36], op=ALU.max
+        )
+
+        for t in range(4):
+            stage1(new_bank(("z", 0, t))[:], 0, t, WIDE)
+            evac_h(banks[("z", 0, t)][:], 0, t, WIDE)
+            if t == 0:
+                group_vt(0, 0)
+                permute_p(1, 0, 4)
+                quantize_vt(0, 0)
+            if t == 1:
+                group_vt(0, 1, on_scalar=True, part=0)
+                group_vt(0, 1, part=1)
+        group_vt(1, 0)
+        quantize_vt(0, 1)
+        group_h(0, WIDE)
+        quantize_vt(1, 0)
+        quantize_h(0, WIDE)
+        nc.scalar.activation(
+            out=vec_f32[0:12, :, :], in_=vec_rows[0:12, :].rearrange("v (m t) -> v t m", t=4), func=ACT.Copy
+        )
+        for t in range(4):
+            stage1(new_bank(("z", 1, t))[:], 1, t, WIDE)
+            evac_h(banks[("z", 1, t)][:], 1, t, WIDE)
+            if t == 1:
+                group_vt(1, 1, on_scalar=True, part=0)
+        group_vt(1, 1, part=1)
+        group_vt(3, 0, part=0)
+        turn_vectors("vec_n", 0, 12)
+        group_h(1, WIDE)
+        quantize_vt(1, 1)
+        quantize_h(1, WIDE)
+        nc.vector.tensor_tensor(out=gain[:], in0=vec_cols[:, :, 0:4], in1=vec_cols[:, :, 4:8], op=ALU.mult)
+        nc.vector.tensor_scalar(
+            out=neg_mu[:], in0=vec_cols[:, :, 8:12], scalar1=-1.0, scalar2=None, op0=ALU.mult
+        )
+
+        for half in range(2):
+            for pair in range(2):
+                bank = new_bank(("zn", half, pair))
+                for s in range(2):
+                    stage1(bank[:, 256 * s : 256 * (s + 1)], half, 2 * pair + s, NARROW)
+                if pair == 0:
+                    group_vt(2, 0, on_scalar=True, part=half)
+                for s in range(2):
+                    evac_h(bank[:, 256 * s : 256 * (s + 1)], half, 2 * pair + s, NARROW)
+            if half == 0:
+                group_vt(3, 0, part=1)
+                group_h(0, NARROW)
+                quantize_vt(3, 0)
+                quantize_h(0, NARROW)
+            else:
+                group_vt(2, 1, part=0)
+                group_h(1, NARROW)
+                quantize_vt(2, 0)
+                quantize_h(1, NARROW)
+
+        on_s = {0: (1, 3, 5), 1: (1, 3, 5), 2: (1, 3, 5), 3: (0, 1, 2, 4)}
+        for g in range(4):
+            y_t[g] = ring.tile([P, 4, B], F32, name="y_t", bufs=3, align_bytes=64)
+            y_rows[g] = ring.tile([P, 6, 512], F32, name="y_rows", align_bytes=64)
+            for t in range(4):
+                stage2(new_bank(("g", g, t))[:], g, t, WIDE)
+                evac_y(banks[("g", g, t)][:], g, t, WIDE)
+            for pair in range(2):
+                bank = new_bank(("gn", g, pair))
+                for s in range(2):
+                    stage2(bank[:, 256 * s : 256 * (s + 1)], g, 2 * pair + s, NARROW)
+                for s in range(2):
+                    evac_y(bank[:, 256 * s : 256 * (s + 1)], g, 2 * pair + s, NARROW)
+            if g == 0:
+                group_vt(2, 1, part=1)
+                group_vt(3, 1)
+                quantize_vt(2, 1)
+                quantize_vt(3, 1)
+            else:
+                group_y(g - 1, WIDE)
+                group_y(g - 1, NARROW)
+                quantize_y(g - 1, WIDE)
+                quantize_y(g - 1, NARROW)
+                store_codes(g - 1)
+                if g == 3:
+                    store_scales(0, 3)
+                    group_y(3, WIDE)
+                    group_y(3, NARROW)
+                    quantize_y(3, WIDE)
+            for j in range(6):
+                turn_y(g, j)
+                evac_turned(g, j, on_scalar=(j in on_s[g]))
+                if g == 3 and j == 3:
+                    quantize_y(3, NARROW)
+                if g < 3 and j % 2 == 1:
+                    store_y(g, j - 1, j + 1)
+                if g == 3:
+                    store_y(g, j, j + 1)
+                if g == 3 and j == 4:
+                    store_codes(3)
+                    store_scales(3, 4)

@@ -31,16 +31,22 @@ def tile_clipped_correlation_risk_gradient_k5_kernel(
         psum = ctx.enter_context(tc.psum_pool(name="psum", bufs=8))
         ctx.enter_context(tc.manual_schedule())
 
-        x_codes = keep.tile([P, 4, 2 * B], U8, align_bytes=64)
+        x_codes = {
+            cols.start: keep.tile([P, 4, 2 * (cols.stop - cols.start)], U8, name="x_codes%d" % cols.start, align_bytes=64)
+            for cols in (WIDE, NARROW)
+        }
         x_plane = keep.tile([P, 4, B], U8, align_bytes=64)
-        p_raw = keep.tile([P, 4, 2 * E], U8, align_bytes=64)
+        p_raw = [keep.tile([P, 4, E], U8, name="p_raw%d" % half, align_bytes=64) for half in range(2)]
         p_raw_plane = keep.tile([P, 4, E], U8, align_bytes=64)
-        p_codes = keep.tile([P, 4, 8, 2 * P], U8, align_bytes=64)
-        p_plane = keep.tile([P, 4, 8, P], U8, align_bytes=64)
-        vt_raw = keep.tile([P, 2, 4, N], BF16, align_bytes=64)
+        p_codes = keep.tile([P, 8, 4, 2 * P], U8, align_bytes=64)
+        p_plane = keep.tile([P, 8, 4, P], U8, align_bytes=64)
+        vt_raw = {}
         vt_codes = keep.tile([P, 4, 2, 512], U32, align_bytes=64)
         vt_plane = keep.tile([P, 4, 2, 512], U8, align_bytes=64)
-        h_rows = keep.tile([P, 2, 4, B], BF16, align_bytes=64)
+        h_rows = {
+            cols.start: keep.tile([P, 2, 4, cols.stop - cols.start], BF16, name="h_rows%d" % cols.start, align_bytes=64)
+            for cols in (WIDE, NARROW)
+        }
         h_grouped = keep.tile([P, 2, B, 4], BF16, align_bytes=64)
         h_codes = keep.tile([P, 2, B], U32, align_bytes=64)
         h_plane = keep.tile([P, 2, B], U8, align_bytes=64)
@@ -66,7 +72,7 @@ def tile_clipped_correlation_risk_gradient_k5_kernel(
 
         def load_words(dst, src, lo, hi):
             nc.sync.dma_start(
-                out=dst[:].bitcast(I32)[:, :, lo:hi],
+                out=dst[:].bitcast(I32),
                 in_=src.bitcast(I32).rearrange("g p w -> p g w")[:, :, lo:hi],
             )
 
@@ -78,26 +84,32 @@ def tile_clipped_correlation_risk_gradient_k5_kernel(
 
         def load_vt(half, lo, hi):
             rows = vt[512 * half : 512 * (half + 1), lo:hi].rearrange("(q t b) n -> b q t n", t=4, b=4)
+            raw = keep.tile([P, 4, hi - lo], BF16, name="vt_raw%d_%d" % (half, lo), align_bytes=64)
+            for g in range(lo // 512, hi // 512):
+                vt_raw[(g, half)] = raw[:, :, 512 * g - lo : 512 * (g + 1) - lo]
             for b in range(4):
-                nc.sync.dma_start(out=vt_raw[b:P:4, half, :, lo:hi], in_=rows[b])
+                nc.sync.dma_start(out=raw[b:P:4, :, :], in_=rows[b])
 
         def permute_p(half, t0, t1):
             tiles = slice(4 * half + t0, 4 * half + t1)
-            words = p_raw[:].bitcast(I32).rearrange("p k (h q t w) -> p k h t q w", h=2, t=4, w=2)
+            words = p_raw[half][:].bitcast(I32).rearrange("p k (q t w) -> p t k q w", t=4, w=2)
             nc.vector.tensor_copy(
-                out=p_codes[:].bitcast(I32)[:, :, tiles, :].rearrange("p k t (q w) -> p k t q w", w=2),
-                in_=words[:, :, half, t0:t1, :, :],
+                out=p_codes[:].bitcast(I32)[:, tiles, :, :].rearrange("p t k (q w) -> p t k q w", w=2),
+                in_=words[:, t0:t1, :, :, :],
             )
-            quads = p_raw_plane[:].bitcast(I32).rearrange("p k (h q t) -> p k h t q", h=2, t=4)
-            nc.vector.tensor_copy(out=p_plane[:].bitcast(I32)[:, :, tiles, :], in_=quads[:, :, half, t0:t1, :])
+
+        def permute_p_plane(half, t0, t1):
+            tiles = slice(4 * half + t0, 4 * half + t1)
+            quads = p_raw_plane[:].bitcast(I32).rearrange("p k (h q t) -> p h t k q", h=2, t=4)
+            nc.vector.tensor_copy(out=p_plane[:].bitcast(I32)[:, tiles, :, :], in_=quads[:, half, t0:t1, :, :])
 
         def stage1(acc, half, t, cols):
             for k in range(4):
                 nc.tensor.matmul_mx(
                     out=acc,
-                    lhsT=p_codes[:, k, 4 * half + t, :].bitcast(FP4X4),
-                    lhsT_scale=p_plane[:, k, 4 * half + t, :],
-                    rhs=x_codes[:, k, 2 * cols.start : 2 * cols.stop].bitcast(FP4X4),
+                    lhsT=p_codes[:, 4 * half + t, k, :].bitcast(FP4X4),
+                    lhsT_scale=p_plane[:, 4 * half + t, k, :],
+                    rhs=x_codes[cols.start][:, k, :].bitcast(FP4X4),
                     rhs_scale=x_plane[:, k, cols],
                     start=(k == 0),
                     stop=(k == 3),
@@ -105,7 +117,7 @@ def tile_clipped_correlation_risk_gradient_k5_kernel(
 
         def evac_h(acc, half, t, cols):
             nc.scalar.activation(
-                out=h_rows[:, half, t, cols], in_=acc, func=ACT.Copy, scale=lam_floored[:, t, half : half + 1]
+                out=h_rows[cols.start][:, half, t, :], in_=acc, func=ACT.Copy, scale=lam_floored[:, t, half : half + 1]
             )
 
         def interleave(dst, src):
@@ -117,7 +129,7 @@ def tile_clipped_correlation_risk_gradient_k5_kernel(
             nc.vector.quantize_mx(out=codes.bitcast(FP8X4), scales=plane, in_=grouped)
 
         def group_h(half, cols):
-            interleave(h_grouped[:, half, cols, :], h_rows[:, half, :, cols])
+            interleave(h_grouped[:, half, cols, :], h_rows[cols.start][:, half, :, :])
 
         def quantize_h(half, cols):
             quantize(
@@ -130,10 +142,10 @@ def tile_clipped_correlation_risk_gradient_k5_kernel(
             if (g, half) not in vt_grouped:
                 vt_grouped[(g, half)] = ring.tile([P, 2048], BF16, name="vt_grouped", bufs=4, align_bytes=64)
             dst = vt_grouped[(g, half)][:].rearrange("p (t a m j) -> p a t j m", t=4, m=2, j=4)
-            src = vt_raw[:, half, :, 512 * g : 512 * (g + 1)].rearrange("p j (a m t) -> p a t j m", m=2, t=4)
+            src = vt_raw[(g, half)].rearrange("p j (a m t) -> p a t j m", m=2, t=4)
             if part is not None:
-                dst = dst[:, 32 * part : 32 * (part + 1)]
-                src = src[:, 32 * part : 32 * (part + 1)]
+                dst = dst[:, :, 2 * part : 2 * (part + 1)]
+                src = src[:, :, 2 * part : 2 * (part + 1)]
             if on_scalar:
                 nc.scalar.copy(out=dst, in_=src)
             else:
@@ -157,7 +169,7 @@ def tile_clipped_correlation_risk_gradient_k5_kernel(
         def evac_y(acc, g, t, cols, on_scalar=True):
             if on_scalar:
                 nc.scalar.activation(
-                    out=y_t[g][:, t, cols],
+                    out=y_t[(g, cols.start)][:, t, :],
                     in_=acc,
                     func=ACT.Identity,
                     scale=gain[:, t, g : g + 1],
@@ -165,7 +177,7 @@ def tile_clipped_correlation_risk_gradient_k5_kernel(
                 )
             else:
                 nc.vector.tensor_scalar(
-                    out=y_t[g][:, t, cols],
+                    out=y_t[(g, cols.start)][:, t, :],
                     in0=acc,
                     scalar1=gain[:, t, g : g + 1],
                     scalar2=neg_mu[:, t, g : g + 1],
@@ -176,7 +188,7 @@ def tile_clipped_correlation_risk_gradient_k5_kernel(
         def group_y(g, cols):
             if g not in y_grouped:
                 y_grouped[g] = ring.tile([P, B, 4], BF16, name="y_grouped", align_bytes=64)
-            interleave(y_grouped[g][:, cols, :], y_t[g][:, :, cols])
+            interleave(y_grouped[g][:, cols, :], y_t[(g, cols.start)][:])
 
         def quantize_y(g, cols):
             quantize(
@@ -185,8 +197,10 @@ def tile_clipped_correlation_risk_gradient_k5_kernel(
 
         def turn_y(g, j):
             bank = new_bank(("turn", g, j))
+            start = WIDE.start if j < 4 else NARROW.start
+            src = y_t[(g, start)][:, :, P * j - start : P * (j + 1) - start]
             for t in range(4):
-                nc.tensor.transpose(bank[:, P * t : P * (t + 1)], y_t[g][:, t, P * j : P * (j + 1)], ident[:])
+                nc.tensor.transpose(bank[:, P * t : P * (t + 1)], src[:, t, :], ident[:])
 
         def evac_turned(g, j, on_scalar):
             dst = y_rows[g][:, j, :].rearrange("p (m t) -> p m t", t=4)
@@ -217,25 +231,23 @@ def tile_clipped_correlation_risk_gradient_k5_kernel(
         nc.vector.memset(p_raw_plane[:].bitcast(I32), 0)
         nc.vector.memset(x_plane[:].bitcast(I32), 0)
         nc.vector.memset(vec_f32[:, 0, :], 0.0)
-        load_words(p_raw, p_words, 0, 256)
-        load_words(x_codes, x_words, 0, 256)
+        make_identity(nc, ident[:])
+        for row, vec in ((32, lam), (34, floor)):
+            nc.sync.dma_start(out=vec_rows[row : row + 2, :], in_=vec.rearrange("(h c) -> h c", c=512))
+        load_words(p_raw[0], p_words, 0, 256)
         for quad in range(4):
             load_scale_rows(nc.sync, p_raw_plane, p_scales, quad)
-        for quad in range(2):
+        load_words(x_codes[0], x_words, 0, 256)
+        for quad in range(4):
             load_scale_rows(nc.sync, x_plane, x_scales, quad)
-        for row, vec in ((32, lam), (34, floor)):
-            nc.gpsimd.dma_start(out=vec_rows[row : row + 2, :], in_=vec.rearrange("(h c) -> h c", c=512))
-        for quad in range(2, 4):
-            load_scale_rows(nc.gpsimd, x_plane, x_scales, quad)
-        make_identity(nc, ident[:])
-        for row, vec in ((0, r), (4, sig), (8, mu)):
-            nc.gpsimd.dma_start(out=vec_rows[row : row + 4, :], in_=vec.rearrange("(g c) -> g c", c=512))
         load_vt(0, 0, 512)
-        load_words(p_raw, p_words, 256, 512)
+        load_words(p_raw[1], p_words, 256, 512)
         load_vt(1, 0, 512)
+        for row, vec in ((0, r), (4, sig), (8, mu)):
+            nc.sync.dma_start(out=vec_rows[row : row + 4, :], in_=vec.rearrange("(g c) -> g c", c=512))
         load_vt(0, 512, 1024)
         load_vt(1, 512, 1024)
-        load_words(x_codes, x_words, 256, 384)
+        load_words(x_codes[512], x_words, 256, 384)
         load_vt(0, 1024, 2048)
         load_vt(1, 1024, 2048)
 
@@ -257,6 +269,9 @@ def tile_clipped_correlation_risk_gradient_k5_kernel(
         turn_vectors("vec_e", 32, 36)
         permute_p(0, 0, 1)
         permute_p(0, 1, 4)
+        permute_p_plane(0, 0, 1)
+        permute_p_plane(0, 1, 4)
+        permute_p_plane(1, 0, 4)
         nc.vector.tensor_tensor(
             out=lam_floored[:], in0=vec_cols[:, :, 32:34], in1=vec_cols[:, :, 34:36], op=ALU.max
         )
@@ -271,8 +286,8 @@ def tile_clipped_correlation_risk_gradient_k5_kernel(
             if t == 1:
                 group_vt(0, 1, on_scalar=True, part=0)
                 group_vt(0, 1, part=1)
-        group_vt(1, 0)
         quantize_vt(0, 1)
+        group_vt(1, 0)
         group_h(0, WIDE)
         quantize_vt(1, 0)
         quantize_h(0, WIDE)
@@ -305,19 +320,19 @@ def tile_clipped_correlation_risk_gradient_k5_kernel(
                 for s in range(2):
                     evac_h(bank[:, 256 * s : 256 * (s + 1)], half, 2 * pair + s, NARROW)
             if half == 0:
-                group_vt(3, 0, part=1)
                 group_h(0, NARROW)
-                quantize_vt(3, 0)
+                group_vt(3, 0, part=1)
                 quantize_h(0, NARROW)
             else:
-                group_vt(2, 1, part=0)
                 group_h(1, NARROW)
-                quantize_vt(2, 0)
+                quantize_vt(3, 0)
                 quantize_h(1, NARROW)
+                quantize_vt(2, 0)
 
-        on_s = {0: (1, 3, 5), 1: (1, 3, 5), 2: (1, 3, 5), 3: (0, 1, 2, 4)}
+        on_s = {0: (0, 1, 3, 5), 1: (1, 3, 5), 2: (1, 3, 5), 3: (0, 1, 2, 4)}
         for g in range(4):
-            y_t[g] = ring.tile([P, 4, B], F32, name="y_t", bufs=3, align_bytes=64)
+            y_t[(g, 0)] = ring.tile([P, 4, 512], F32, name="y_t_wide", bufs=3, align_bytes=64)
+            y_t[(g, 512)] = ring.tile([P, 4, 256], F32, name="y_t_narrow", bufs=3, align_bytes=64)
             y_rows[g] = ring.tile([P, 6, 512], F32, name="y_rows", align_bytes=64)
             for t in range(4):
                 stage2(new_bank(("g", g, t))[:], g, t, WIDE)
@@ -329,7 +344,7 @@ def tile_clipped_correlation_risk_gradient_k5_kernel(
                 for s in range(2):
                     evac_y(bank[:, 256 * s : 256 * (s + 1)], g, 2 * pair + s, NARROW)
             if g == 0:
-                group_vt(2, 1, part=1)
+                group_vt(2, 1)
                 group_vt(3, 1)
                 quantize_vt(2, 1)
                 quantize_vt(3, 1)

@@ -76,10 +76,10 @@ def tile_clipped_correlation_risk_gradient_k5_kernel(
                 in_=src.bitcast(I32).rearrange("g p w -> p g w")[:, :, lo:hi],
             )
 
-        def load_scale_rows(eng, dst, src, quad):
+        def load_scale_rows(eng, dst, src, row):
             eng.dma_start(
-                out=dst[:].bitcast(I32)[32 * quad : 32 * quad + 4, :, :],
-                in_=src.bitcast(I32)[:, 4 * quad : 4 * quad + 4, :].rearrange("g r w -> r g w"),
+                out=dst[:].bitcast(I32)[row:P:32, :, :],
+                in_=src.bitcast(I32)[:, row:16:4, :].rearrange("g q w -> q g w"),
             )
 
         def load_vt(half, lo, hi):
@@ -115,10 +115,13 @@ def tile_clipped_correlation_risk_gradient_k5_kernel(
                     stop=(k == 3),
                 )
 
-        def evac_h(acc, half, t, cols):
-            nc.scalar.activation(
-                out=h_rows[cols.start][:, half, t, :], in_=acc, func=ACT.Copy, scale=lam_floored[:, t, half : half + 1]
-            )
+        def evac_h(acc, half, t, cols, on_scalar=True):
+            dst = h_rows[cols.start][:, half, t, :]
+            factor = lam_floored[:, t, half : half + 1]
+            if on_scalar:
+                nc.scalar.activation(out=dst, in_=acc, func=ACT.Copy, scale=factor)
+            else:
+                nc.vector.tensor_scalar(out=dst, in0=acc, scalar1=factor, scalar2=None, op0=ALU.mult)
 
         def interleave(dst, src):
             nc.vector.tensor_copy(
@@ -186,13 +189,17 @@ def tile_clipped_correlation_risk_gradient_k5_kernel(
                 )
 
         def group_y(g, cols):
-            if g not in y_grouped:
-                y_grouped[g] = ring.tile([P, B, 4], BF16, name="y_grouped", align_bytes=64)
-            interleave(y_grouped[g][:, cols, :], y_t[(g, cols.start)][:])
+            width = cols.stop - cols.start
+            y_grouped[(g, cols.start)] = ring.tile(
+                [P, width, 4], BF16, name="y_grouped%d" % width, align_bytes=64
+            )
+            interleave(y_grouped[(g, cols.start)][:], y_t[(g, cols.start)][:])
 
         def quantize_y(g, cols):
             quantize(
-                y_codes[:, g, cols], y_plane[:, g, cols], y_grouped[g][:, cols, :].rearrange("p b t -> p (b t)")
+                y_codes[:, g, cols],
+                y_plane[:, g, cols],
+                y_grouped[(g, cols.start)][:].rearrange("p b t -> p (b t)"),
             )
 
         def turn_y(g, j):
@@ -203,7 +210,7 @@ def tile_clipped_correlation_risk_gradient_k5_kernel(
                 nc.tensor.transpose(bank[:, P * t : P * (t + 1)], src[:, t, :], ident[:])
 
         def evac_turned(g, j, on_scalar):
-            dst = y_rows[g][:, j, :].rearrange("p (m t) -> p m t", t=4)
+            dst = y_rows[(g, j - j % 2)][:, j % 2, :].rearrange("p (m t) -> p m t", t=4)
             src = banks[("turn", g, j)][:].rearrange("p (t m) -> p m t", t=4)
             if on_scalar:
                 nc.scalar.copy(out=dst, in_=src)
@@ -213,19 +220,20 @@ def tile_clipped_correlation_risk_gradient_k5_kernel(
         def store_y(g, j0, j1):
             nc.sync.dma_start(
                 out=out_0[P * j0 : P * j1, 512 * g : 512 * (g + 1)].rearrange("(j p) n -> p j n", p=P),
-                in_=y_rows[g][:, j0:j1, :],
+                in_=y_rows[(g, j0)][:],
             )
 
-        def store_codes(g):
+        def store_codes(g, cols):
             nc.sync.dma_start(
-                out=out_1[g].rearrange("p m t -> p (m t)").bitcast(I32), in_=y_codes[:, g, :].bitcast(I32)
+                out=out_1[g].rearrange("p m t -> p (m t)").bitcast(I32)[:, cols],
+                in_=y_codes[:, g, cols].bitcast(I32),
             )
 
         def store_scales(g0, g1):
-            for quad in range(4):
+            for row in range(4):
                 nc.sync.dma_start(
-                    out=out_2.bitcast(I32)[g0:g1, 4 * quad : 4 * quad + 4, :].rearrange("g r w -> r g w"),
-                    in_=y_plane[:].bitcast(I32)[32 * quad : 32 * quad + 4, g0:g1, :],
+                    out=out_2.bitcast(I32)[g0:g1, row:16:4, :].rearrange("g q w -> q g w"),
+                    in_=y_plane[:].bitcast(I32)[row:P:32, g0:g1, :],
                 )
 
         nc.vector.memset(p_raw_plane[:].bitcast(I32), 0)
@@ -234,30 +242,22 @@ def tile_clipped_correlation_risk_gradient_k5_kernel(
         make_identity(nc, ident[:])
         for row, vec in ((32, lam), (34, floor)):
             nc.sync.dma_start(out=vec_rows[row : row + 2, :], in_=vec.rearrange("(h c) -> h c", c=512))
+        for row, vec in ((0, r), (4, sig), (8, mu)):
+            nc.sync.dma_start(out=vec_rows[row : row + 4, :], in_=vec.rearrange("(g c) -> g c", c=512))
         load_words(p_raw[0], p_words, 0, 256)
-        for quad in range(4):
-            load_scale_rows(nc.sync, p_raw_plane, p_scales, quad)
+        for row in range(4):
+            load_scale_rows(nc.sync, p_raw_plane, p_scales, row)
         load_words(x_codes[0], x_words, 0, 256)
-        for quad in range(4):
-            load_scale_rows(nc.sync, x_plane, x_scales, quad)
+        for row in range(4):
+            load_scale_rows(nc.sync, x_plane, x_scales, row)
         load_vt(0, 0, 512)
         load_words(p_raw[1], p_words, 256, 512)
         load_vt(1, 0, 512)
-        for row, vec in ((0, r), (4, sig), (8, mu)):
-            nc.sync.dma_start(out=vec_rows[row : row + 4, :], in_=vec.rearrange("(g c) -> g c", c=512))
         load_vt(0, 512, 1024)
         load_vt(1, 512, 1024)
         load_words(x_codes[512], x_words, 256, 384)
         load_vt(0, 1024, 2048)
         load_vt(1, 1024, 2048)
-
-        def turn_vectors(key, lo, hi):
-            bank = new_bank(key)
-            for t in range(4):
-                nc.tensor.transpose(bank[:, P * t : P * (t + 1)], vec_f32[:, t, :], ident[:])
-            nc.scalar.copy(
-                out=vec_cols[:, :, lo:hi], in_=bank[:].rearrange("p (t v) -> p t v", t=4)[:, :, lo:hi]
-            )
 
         for t in range(1, 4):
             nc.scalar.activation(out=vec_f32[:, t, :], in_=vec_f32[:, 0, :], func=ACT.Copy)
@@ -266,108 +266,145 @@ def tile_clipped_correlation_risk_gradient_k5_kernel(
             in_=vec_rows[32:36, :].rearrange("v (q t b) -> v t q b", t=4, b=4),
             func=ACT.Copy,
         )
-        turn_vectors("vec_e", 32, 36)
-        permute_p(0, 0, 1)
-        permute_p(0, 1, 4)
-        permute_p_plane(0, 0, 1)
-        permute_p_plane(0, 1, 4)
+        nc.scalar.activation(
+            out=vec_f32[0:12, :, :], in_=vec_rows[0:12, :].rearrange("v (m t) -> v t m", t=4), func=ACT.Copy
+        )
+        vec_bank = new_bank("vec")
+        for t in range(4):
+            nc.tensor.transpose(vec_bank[:, P * t : P * (t + 1)], vec_f32[:, t, :], ident[:])
+        nc.scalar.copy(out=vec_cols[:], in_=vec_bank[:].rearrange("p (t v) -> p t v", t=4)[:, :, 0:36])
+        permute_p(0, 0, 2)
+        permute_p_plane(0, 0, 2)
+        permute_p(0, 2, 4)
+        permute_p_plane(0, 2, 4)
         permute_p_plane(1, 0, 4)
         nc.vector.tensor_tensor(
             out=lam_floored[:], in0=vec_cols[:, :, 32:34], in1=vec_cols[:, :, 34:36], op=ALU.max
         )
-
-        for t in range(4):
-            stage1(new_bank(("z", 0, t))[:], 0, t, WIDE)
-            evac_h(banks[("z", 0, t)][:], 0, t, WIDE)
-            if t == 0:
-                group_vt(0, 0)
-                permute_p(1, 0, 4)
-                quantize_vt(0, 0)
-            if t == 1:
-                group_vt(0, 1, on_scalar=True, part=0)
-                group_vt(0, 1, part=1)
-        quantize_vt(0, 1)
-        group_vt(1, 0)
-        group_h(0, WIDE)
-        quantize_vt(1, 0)
-        quantize_h(0, WIDE)
-        nc.scalar.activation(
-            out=vec_f32[0:12, :, :], in_=vec_rows[0:12, :].rearrange("v (m t) -> v t m", t=4), func=ACT.Copy
-        )
-        for t in range(4):
-            stage1(new_bank(("z", 1, t))[:], 1, t, WIDE)
-            evac_h(banks[("z", 1, t)][:], 1, t, WIDE)
-            if t == 1:
-                group_vt(1, 1, on_scalar=True, part=0)
-        group_vt(1, 1, part=1)
-        group_vt(3, 0, part=0)
-        turn_vectors("vec_n", 0, 12)
-        group_h(1, WIDE)
-        quantize_vt(1, 1)
-        quantize_h(1, WIDE)
         nc.vector.tensor_tensor(out=gain[:], in0=vec_cols[:, :, 0:4], in1=vec_cols[:, :, 4:8], op=ALU.mult)
         nc.vector.tensor_scalar(
             out=neg_mu[:], in0=vec_cols[:, :, 8:12], scalar1=-1.0, scalar2=None, op0=ALU.mult
         )
 
-        for half in range(2):
+        def z_narrow(half, on_vector=()):
             for pair in range(2):
                 bank = new_bank(("zn", half, pair))
                 for s in range(2):
                     stage1(bank[:, 256 * s : 256 * (s + 1)], half, 2 * pair + s, NARROW)
-                if pair == 0:
-                    group_vt(2, 0, on_scalar=True, part=half)
                 for s in range(2):
-                    evac_h(bank[:, 256 * s : 256 * (s + 1)], half, 2 * pair + s, NARROW)
-            if half == 0:
-                group_h(0, NARROW)
-                group_vt(3, 0, part=1)
-                quantize_h(0, NARROW)
-            else:
-                group_h(1, NARROW)
-                quantize_vt(3, 0)
-                quantize_h(1, NARROW)
-                quantize_vt(2, 0)
+                    evac_h(bank[:, 256 * s : 256 * (s + 1)], half, 2 * pair + s, NARROW, 2 * pair + s not in on_vector)
 
-        on_s = {0: (0, 1, 3, 5), 1: (1, 3, 5), 2: (1, 3, 5), 3: (0, 1, 2, 4)}
-        for g in range(4):
-            y_t[(g, 0)] = ring.tile([P, 4, 512], F32, name="y_t_wide", bufs=3, align_bytes=64)
+        def z_wide(half, t):
+            stage1(new_bank(("z", half, t))[:], half, t, WIDE)
+            evac_h(banks[("z", half, t)][:], half, t, WIDE)
+
+        def g_narrow(g):
             y_t[(g, 512)] = ring.tile([P, 4, 256], F32, name="y_t_narrow", bufs=3, align_bytes=64)
-            y_rows[g] = ring.tile([P, 6, 512], F32, name="y_rows", align_bytes=64)
-            for t in range(4):
-                stage2(new_bank(("g", g, t))[:], g, t, WIDE)
-                evac_y(banks[("g", g, t)][:], g, t, WIDE)
             for pair in range(2):
                 bank = new_bank(("gn", g, pair))
                 for s in range(2):
                     stage2(bank[:, 256 * s : 256 * (s + 1)], g, 2 * pair + s, NARROW)
                 for s in range(2):
                     evac_y(bank[:, 256 * s : 256 * (s + 1)], g, 2 * pair + s, NARROW)
-            if g == 0:
-                group_vt(2, 1)
-                group_vt(3, 1)
-                quantize_vt(2, 1)
-                quantize_vt(3, 1)
-            else:
-                group_y(g - 1, WIDE)
-                group_y(g - 1, NARROW)
-                quantize_y(g - 1, WIDE)
-                quantize_y(g - 1, NARROW)
-                store_codes(g - 1)
-                if g == 3:
-                    store_scales(0, 3)
-                    group_y(3, WIDE)
-                    group_y(3, NARROW)
-                    quantize_y(3, WIDE)
-            for j in range(6):
-                turn_y(g, j)
-                evac_turned(g, j, on_scalar=(j in on_s[g]))
-                if g == 3 and j == 3:
-                    quantize_y(3, NARROW)
-                if g < 3 and j % 2 == 1:
-                    store_y(g, j - 1, j + 1)
-                if g == 3:
-                    store_y(g, j, j + 1)
-                if g == 3 and j == 4:
-                    store_codes(3)
-                    store_scales(3, 4)
+
+        def g_wide(g, on_vector=()):
+            y_t[(g, 0)] = ring.tile([P, 4, 512], F32, name="y_t_wide", bufs=3, align_bytes=64)
+            for t in range(4):
+                stage2(new_bank(("g", g, t))[:], g, t, WIDE)
+                evac_y(banks[("g", g, t)][:], g, t, WIDE, t not in on_vector)
+
+        def turn(g, j, on_scalar=True):
+            if j % 2 == 0:
+                y_rows[(g, j)] = ring.tile([P, 2, 512], F32, name="y_rows", bufs=6, align_bytes=64)
+            turn_y(g, j)
+            evac_turned(g, j, on_scalar)
+            if j % 2 == 1:
+                store_y(g, j - 1, j + 1)
+
+        def vt_unit(g, half, s0=False):
+            group_vt(g, half, on_scalar=s0, part=0)
+            group_vt(g, half, part=1)
+
+        def y_planes(g, cols):
+            group_y(g, cols)
+            quantize_y(g, cols)
+            store_codes(g, cols)
+
+        z_wide(0, 0)
+        vt_unit(0, 0, True)
+        permute_p(1, 0, 4)
+        quantize_vt(0, 0)
+        z_wide(0, 1)
+        z_wide(0, 2)
+        z_wide(0, 3)
+        vt_unit(0, 1, True)
+        group_h(0, WIDE)
+        group_vt(1, 0)
+        z_wide(1, 0)
+        z_wide(1, 1)
+        vt_unit(1, 1, True)
+        quantize_vt(0, 1)
+        quantize_h(0, WIDE)
+        quantize_vt(1, 1)
+        z_wide(1, 2)
+        z_wide(1, 3)
+        group_h(1, WIDE)
+        group_vt(3, 0)
+        quantize_h(1, WIDE)
+        quantize_vt(1, 0)
+        z_narrow(0)
+        group_vt(2, 0, on_scalar=True, part=0)
+        group_h(0, NARROW)
+        z_narrow(1)
+        group_h(1, NARROW)
+        quantize_h(0, NARROW)
+        quantize_h(1, NARROW)
+        g_wide(0)
+        g_narrow(0)
+        group_vt(2, 0, part=1)
+        group_vt(2, 1)
+        group_y(0, WIDE)
+        group_y(0, NARROW)
+        for j in range(6):
+            turn(0, j, j not in (2, 4))
+            if j == 2:
+                quantize_y(0, WIDE)
+                quantize_y(0, NARROW)
+                store_codes(0, slice(0, B))
+        quantize_vt(2, 0)
+        quantize_vt(2, 1)
+        g_wide(1)
+        g_narrow(1)
+        group_y(1, WIDE)
+        for j in range(6):
+            turn(1, j, j not in (2, 4))
+            if j == 2:
+                group_y(1, NARROW)
+        quantize_y(1, WIDE)
+        quantize_y(1, NARROW)
+        store_codes(1, slice(0, B))
+        group_vt(3, 1)
+        quantize_vt(3, 0)
+        quantize_vt(3, 1)
+        g_wide(2)
+        g_narrow(2)
+        for j in range(6):
+            turn(2, j, j not in (2, 4))
+            if j == 2:
+                group_y(2, NARROW)
+        group_y(2, WIDE)
+        quantize_y(2, NARROW)
+        quantize_y(2, WIDE)
+        store_codes(2, slice(0, B))
+        store_scales(0, 3)
+        g_wide(3)
+        g_narrow(3)
+        group_y(3, WIDE)
+        for j in range(6):
+            turn(3, j, j not in (1,))
+            if j == 1:
+                group_y(3, NARROW)
+                quantize_y(3, WIDE)
+                quantize_y(3, NARROW)
+        store_codes(3, slice(0, B))
+        store_scales(3, 4)

@@ -236,9 +236,9 @@ def tile_clipped_correlation_risk_gradient_k5_kernel(
                     in_=y_plane[:].bitcast(I32)[row:P:32, g0:g1, :],
                 )
 
+        nc.vector.memset(vec_f32[:, 0, :], 0.0)
         nc.vector.memset(p_raw_plane[:].bitcast(I32), 0)
         nc.vector.memset(x_plane[:].bitcast(I32), 0)
-        nc.vector.memset(vec_f32[:, 0, :], 0.0)
         make_identity(nc, ident[:])
         for row, vec in ((32, lam), (34, floor)):
             nc.sync.dma_start(out=vec_rows[row : row + 2, :], in_=vec.rearrange("(h c) -> h c", c=512))
@@ -266,15 +266,24 @@ def tile_clipped_correlation_risk_gradient_k5_kernel(
             in_=vec_rows[32:36, :].rearrange("v (q t b) -> v t q b", t=4, b=4),
             func=ACT.Copy,
         )
-        nc.scalar.activation(
-            out=vec_f32[0:12, :, :], in_=vec_rows[0:12, :].rearrange("v (m t) -> v t m", t=4), func=ACT.Copy
-        )
+        nc.vector.tensor_copy(out=vec_f32[0:12, :, :], in_=vec_rows[0:12, :].rearrange("v (m t) -> v t m", t=4))
         vec_bank = new_bank("vec")
         for t in range(4):
             nc.tensor.transpose(vec_bank[:, P * t : P * (t + 1)], vec_f32[:, t, :], ident[:])
         nc.scalar.copy(out=vec_cols[:], in_=vec_bank[:].rearrange("p (t v) -> p t v", t=4)[:, :, 0:36])
         permute_p(0, 0, 2)
         permute_p_plane(0, 0, 2)
+        warm = new_bank("warm")
+        for i in range(2):
+            nc.tensor.matmul_mx(
+                out=warm[:],
+                lhsT=p_codes[:, 0, 0, :].bitcast(FP4X4),
+                lhsT_scale=p_plane[:, 0, 0, :],
+                rhs=p_codes[:, 0, :, :].rearrange("p k c -> p (k c)").bitcast(FP4X4),
+                rhs_scale=p_plane[:, 0, :, :].rearrange("p k c -> p (k c)"),
+                start=True,
+                stop=True,
+            )
         permute_p(0, 2, 4)
         permute_p_plane(0, 2, 4)
         permute_p_plane(1, 0, 4)

@@ -250,11 +250,9 @@ def tile_clipped_correlation_risk_gradient_k5_kernel(
         load_words(x_codes[0], x_words, 0, 256)
         for row in range(4):
             load_scale_rows(nc.sync, x_plane, x_scales, row)
-        load_vt(0, 0, 512)
+        load_vt(0, 0, 1024)
         load_words(p_raw[1], p_words, 256, 512)
-        load_vt(1, 0, 512)
-        load_vt(0, 512, 1024)
-        load_vt(1, 512, 1024)
+        load_vt(1, 0, 1024)
         load_words(x_codes[512], x_words, 256, 384)
         load_vt(0, 1024, 2048)
         load_vt(1, 1024, 2048)
@@ -274,7 +272,7 @@ def tile_clipped_correlation_risk_gradient_k5_kernel(
         permute_p(0, 0, 2)
         permute_p_plane(0, 0, 2)
         warm = new_bank("warm")
-        for i in range(2):
+        for i in range(3):
             nc.tensor.matmul_mx(
                 out=warm[:],
                 lhsT=p_codes[:, 0, 0, :].bitcast(FP4X4),
@@ -307,14 +305,14 @@ def tile_clipped_correlation_risk_gradient_k5_kernel(
             stage1(new_bank(("z", half, t))[:], half, t, WIDE)
             evac_h(banks[("z", half, t)][:], half, t, WIDE)
 
-        def g_narrow(g):
+        def g_narrow(g, on_vector=()):
             y_t[(g, 512)] = ring.tile([P, 4, 256], F32, name="y_t_narrow", bufs=3, align_bytes=64)
             for pair in range(2):
                 bank = new_bank(("gn", g, pair))
                 for s in range(2):
                     stage2(bank[:, 256 * s : 256 * (s + 1)], g, 2 * pair + s, NARROW)
                 for s in range(2):
-                    evac_y(bank[:, 256 * s : 256 * (s + 1)], g, 2 * pair + s, NARROW)
+                    evac_y(bank[:, 256 * s : 256 * (s + 1)], g, 2 * pair + s, NARROW, 2 * pair + s not in on_vector)
 
         def g_wide(g, on_vector=()):
             y_t[(g, 0)] = ring.tile([P, 4, 512], F32, name="y_t_wide", bufs=3, align_bytes=64)
@@ -340,29 +338,30 @@ def tile_clipped_correlation_risk_gradient_k5_kernel(
             store_codes(g, cols)
 
         z_wide(0, 0)
-        vt_unit(0, 0, True)
+        group_vt(0, 0)
         permute_p(1, 0, 4)
-        quantize_vt(0, 0)
         z_wide(0, 1)
+        vt_unit(1, 0, True)
+        quantize_vt(0, 0)
         z_wide(0, 2)
         z_wide(0, 3)
-        vt_unit(0, 1, True)
+        quantize_vt(1, 0)
         group_h(0, WIDE)
-        group_vt(1, 0)
         z_wide(1, 0)
         z_wide(1, 1)
+        group_vt(0, 1)
+        quantize_h(0, WIDE)
         vt_unit(1, 1, True)
         quantize_vt(0, 1)
-        quantize_h(0, WIDE)
-        quantize_vt(1, 1)
         z_wide(1, 2)
         z_wide(1, 3)
         group_h(1, WIDE)
-        group_vt(3, 0)
+        quantize_vt(1, 1)
         quantize_h(1, WIDE)
-        quantize_vt(1, 0)
+        group_vt(3, 0, on_scalar=True, part=0)
         z_narrow(0)
         group_vt(2, 0, on_scalar=True, part=0)
+        group_vt(3, 0, part=1)
         group_h(0, NARROW)
         z_narrow(1)
         group_h(1, NARROW)

from contextlib import ExitStack

import concourse.mybir as mybir
from concourse.masks import make_identity

B, N, E = 768, 2048, 1024
FLOPS = 2 * B * N * E * 2

F32 = mybir.dt.float32
BF16 = mybir.dt.bfloat16
I32 = mybir.dt.int32
U32 = mybir.dt.uint32
U8 = mybir.dt.uint8
FP8X4 = mybir.dt.float8_e4m3fn_x4
FP4X4 = mybir.dt.float4_e2m1fn_x4
ACT = mybir.ActivationFunctionType
ALU = mybir.AluOpType

P = 128
WIDE = slice(0, 512)
NARROW = slice(512, 768)


def tile_clipped_correlation_risk_gradient_k5_kernel(
    tc, x_words, x_scales, p_words, p_scales, vt, lam, floor, r, sig, mu, out_0, out_1, out_2
):
    nc = tc.nc
    with ExitStack() as ctx:
        keep = ctx.enter_context(tc.tile_pool(name="keep", bufs=1))
        ring = ctx.enter_context(tc.tile_pool(name="ring", bufs=2))
        psum = ctx.enter_context(tc.psum_pool(name="psum", bufs=8))
        ctx.enter_context(tc.manual_schedule())

        x_codes = {
            cols.start: keep.tile([P, 4, 2 * (cols.stop - cols.start)], U8, name="x_codes%d" % cols.start, align_bytes=64)
            for cols in (WIDE, NARROW)
        }
        x_plane = keep.tile([P, 4, B], U8, align_bytes=64)
        p_raw = [keep.tile([P, 4, E], U8, name="p_raw%d" % half, align_bytes=64) for half in range(2)]
        p_raw_plane = keep.tile([P, 4, E], U8, align_bytes=64)
        p_codes = keep.tile([P, 8, 4, 2 * P], U8, align_bytes=64)
        p_plane = keep.tile([P, 8, 4, P], U8, align_bytes=64)
        vt_raw = {}
        vt_codes = keep.tile([P, 4, 2, 512], U32, align_bytes=64)
        vt_plane = keep.tile([P, 4, 2, 512], U8, align_bytes=64)
        h_rows = {
            cols.start: keep.tile([P, 2, 4, cols.stop - cols.start], BF16, name="h_rows%d" % cols.start, align_bytes=64)
            for cols in (WIDE, NARROW)
        }
        h_grouped = keep.tile([P, 2, B, 4], BF16, align_bytes=64)
        h_codes = keep.tile([P, 2, B], U32, align_bytes=64)
        h_plane = keep.tile([P, 2, B], U8, align_bytes=64)
        y_codes = keep.tile([P, 4, B], U32, align_bytes=64)
        y_plane = keep.tile([P, 4, B], U8, align_bytes=64)
        ident = keep.tile([P, P], F32, align_bytes=64)
        vec_rows = keep.tile([P, 512], BF16, align_bytes=64)
        vec_f32 = keep.tile([P, 4, P], F32, align_bytes=64)
        vec_cols = keep.tile([P, 4, 36], F32, align_bytes=64)
        gain = keep.tile([P, 4, 4], F32, align_bytes=64)
        neg_mu = keep.tile([P, 4, 4], F32, align_bytes=64)
        lam_floored = keep.tile([P, 4, 2], F32, align_bytes=64)

        vt_grouped = {}
        y_t = {}
        y_grouped = {}
        y_rows = {}
        banks = {}

        def new_bank(key):
            banks[key] = psum.tile([P, 512], F32, name="bank")
            return banks[key]

        def load_words(dst, src, lo, hi):
            nc.sync.dma_start(
                out=dst[:].bitcast(I32),
                in_=src.bitcast(I32).rearrange("g p w -> p g w")[:, :, lo:hi],
            )

        def load_scale_rows(eng, dst, src, row):
            eng.dma_start(
                out=dst[:].bitcast(I32)[row:P:32, :, :],
                in_=src.bitcast(I32)[:, row:16:4, :].rearrange("g q w -> q g w"),
            )

        def load_vt(half, lo, hi):
            rows = vt[512 * half : 512 * (half + 1), lo:hi].rearrange("(q t b) n -> b q t n", t=4, b=4)
            raw = keep.tile([P, 4, hi - lo], BF16, name="vt_raw%d_%d" % (half, lo), align_bytes=64)
            for g in range(lo // 512, hi // 512):
                vt_raw[(g, half)] = raw[:, :, 512 * g - lo : 512 * (g + 1) - lo]
            for b in range(4):
                nc.sync.dma_start(out=raw[b:P:4, :, :], in_=rows[b])

        def permute_p(half, t0, t1):
            tiles = slice(4 * half + t0, 4 * half + t1)
            words = p_raw[half][:].bitcast(I32).rearrange("p k (q t w) -> p t k q w", t=4, w=2)
            nc.vector.tensor_copy(
                out=p_codes[:].bitcast(I32)[:, tiles, :, :].rearrange("p t k (q w) -> p t k q w", w=2),
                in_=words[:, t0:t1, :, :, :],
            )

        def permute_p_plane(half, t0, t1):
            tiles = slice(4 * half + t0, 4 * half + t1)
            quads = p_raw_plane[:].bitcast(I32).rearrange("p k (h q t) -> p h t k q", h=2, t=4)
            nc.vector.tensor_copy(out=p_plane[:].bitcast(I32)[:, tiles, :, :], in_=quads[:, half, t0:t1, :, :])

        def stage1(acc, half, t, cols):
            for k in range(4):
                nc.tensor.matmul_mx(
                    out=acc,
                    lhsT=p_codes[:, 4 * half + t, k, :].bitcast(FP4X4),
                    lhsT_scale=p_plane[:, 4 * half + t, k, :],
                    rhs=x_codes[cols.start][:, k, :].bitcast(FP4X4),
                    rhs_scale=x_plane[:, k, cols],
                    start=(k == 0),
                    stop=(k == 3),
                )

        def evac_h(acc, half, t, cols, on_scalar=True):
            dst = h_rows[cols.start][:, half, t, :]
            factor = lam_floored[:, t, half : half + 1]
            if on_scalar:
                nc.scalar.activation(out=dst, in_=acc, func=ACT.Copy, scale=factor)
            else:
                nc.vector.tensor_scalar(out=dst, in0=acc, scalar1=factor, scalar2=None, op0=ALU.mult)

        def interleave(dst, src):
            nc.vector.tensor_copy(
                out=dst.rearrange("p (c i) t -> p c t i", i=4), in_=src.rearrange("p t (c i) -> p c t i", i=4)
            )

        def quantize(codes, plane, grouped):
            nc.vector.quantize_mx(out=codes.bitcast(FP8X4), scales=plane, in_=grouped)

        def group_h(half, cols):
            interleave(h_grouped[:, half, cols, :], h_rows[cols.start][:, half, :, :])

        def quantize_h(half, cols):
            quantize(
                h_codes[:, half, cols],
                h_plane[:, half, cols],
                h_grouped[:, half, cols, :].rearrange("p b t -> p (b t)"),
            )

        def group_vt(g, half, on_scalar=False, part=None):
            if (g, half) not in vt_grouped:
                vt_grouped[(g, half)] = ring.tile([P, 2048], BF16, name="vt_grouped", bufs=4, align_bytes=64)
            dst = vt_grouped[(g, half)][:].rearrange("p (t a m j) -> p a t j m", t=4, m=2, j=4)
            src = vt_raw[(g, half)].rearrange("p j (a m t) -> p a t j m", m=2, t=4)
            if part is not None:
                dst = dst[:, :, 2 * part : 2 * (part + 1)]
                src = src[:, :, 2 * part : 2 * (part + 1)]
            if on_scalar:
                nc.scalar.copy(out=dst, in_=src)
            else:
                nc.vector.tensor_copy(out=dst, in_=src)

        def quantize_vt(g, half):
            quantize(vt_codes[:, g, half, :], vt_plane[:, g, half, :], vt_grouped[(g, half)][:])

        def stage2(acc, g, t, cols):
            for half in range(2):
                nc.tensor.matmul_mx(
                    out=acc,
                    lhsT=vt_codes[:, g, half, P * t : P * (t + 1)].bitcast(FP8X4),
                    lhsT_scale=vt_plane[:, g, half, P * t : P * (t + 1)],
                    rhs=h_codes[:, half, cols].bitcast(FP8X4),
                    rhs_scale=h_plane[:, half, cols],
                    start=(half == 0),
                    stop=(half == 1),
                )

        def evac_y(acc, g, t, cols, on_scalar=True):
            if on_scalar:
                nc.scalar.activation(
                    out=y_t[(g, cols.start)][:, t, :],
                    in_=acc,
                    func=ACT.Identity,
                    scale=gain[:, t, g : g + 1],
                    bias=neg_mu[:, t, g : g + 1],
                )
            else:
                nc.vector.tensor_scalar(
                    out=y_t[(g, cols.start)][:, t, :],
                    in0=acc,
                    scalar1=gain[:, t, g : g + 1],
                    scalar2=neg_mu[:, t, g : g + 1],
                    op0=ALU.mult,
                    op1=ALU.add,
                )

        def group_y(g, cols):
            width = cols.stop - cols.start
            y_grouped[(g, cols.start)] = ring.tile(
                [P, width, 4], BF16, name="y_grouped%d" % width, align_bytes=64
            )
            interleave(y_grouped[(g, cols.start)][:], y_t[(g, cols.start)][:])

        def quantize_y(g, cols):
            quantize(
                y_codes[:, g, cols],
                y_plane[:, g, cols],
                y_grouped[(g, cols.start)][:].rearrange("p b t -> p (b t)"),
            )

        def turn_y(g, j):
            bank = new_bank(("turn", g, j))
            start = WIDE.start if j < 4 else NARROW.start
            src = y_t[(g, start)][:, :, P * j - start : P * (j + 1) - start]
            for t in range(4):
                nc.tensor.transpose(bank[:, P * t : P * (t + 1)], src[:, t, :], ident[:])

        def evac_turned(g, j, on_scalar):
            dst = y_rows[(g, j - j % 2)][:, j % 2, :].rearrange("p (m t) -> p m t", t=4)
            src = banks[("turn", g, j)][:].rearrange("p (t m) -> p m t", t=4)
            if on_scalar:
                nc.scalar.copy(out=dst, in_=src)
            else:
                nc.vector.tensor_copy(out=dst, in_=src)

        def store_y(g, j0, j1):
            nc.sync.dma_start(
                out=out_0[P * j0 : P * j1, 512 * g : 512 * (g + 1)].rearrange("(j p) n -> p j n", p=P),
                in_=y_rows[(g, j0)][:],
            )

        def store_codes(g, cols):
            nc.sync.dma_start(
                out=out_1[g].rearrange("p m t -> p (m t)").bitcast(I32)[:, cols],
                in_=y_codes[:, g, cols].bitcast(I32),
            )

        def store_scales(g0, g1):
            for row in range(4):
                nc.sync.dma_start(
                    out=out_2.bitcast(I32)[g0:g1, row:16:4, :].rearrange("g q w -> q g w"),
                    in_=y_plane[:].bitcast(I32)[row:P:32, g0:g1, :],
                )

        nc.vector.memset(vec_f32[:, 0, :], 0.0)
        nc.vector.memset(p_raw_plane[:].bitcast(I32), 0)
        nc.vector.memset(x_plane[:].bitcast(I32), 0)
        make_identity(nc, ident[:])
        for row, vec in ((32, lam), (34, floor)):
            nc.sync.dma_start(out=vec_rows[row : row + 2, :], in_=vec.rearrange("(h c) -> h c", c=512))
        for row, vec in ((0, r), (4, sig), (8, mu)):
            nc.sync.dma_start(out=vec_rows[row : row + 4, :], in_=vec.rearrange("(g c) -> g c", c=512))
        load_words(p_raw[0], p_words, 0, 256)
        for row in range(4):
            load_scale_rows(nc.sync, p_raw_plane, p_scales, row)
        load_words(x_codes[0], x_words, 0, 256)
        for row in range(4):
            load_scale_rows(nc.sync, x_plane, x_scales, row)
        load_vt(0, 0, 1024)
        load_words(p_raw[1], p_words, 256, 512)
        load_vt(1, 0, 1024)
        load_words(x_codes[512], x_words, 256, 384)
        load_vt(0, 1024, 2048)
        load_vt(1, 1024, 2048)

        for t in range(1, 4):
            nc.scalar.activation(out=vec_f32[:, t, :], in_=vec_f32[:, 0, :], func=ACT.Copy)
        nc.scalar.activation(
            out=vec_f32[32:36, :, :].rearrange("v t (q b) -> v t q b", b=4),
            in_=vec_rows[32:36, :].rearrange("v (q t b) -> v t q b", t=4, b=4),
            func=ACT.Copy,
        )
        nc.vector.tensor_copy(out=vec_f32[0:12, :, :], in_=vec_rows[0:12, :].rearrange("v (m t) -> v t m", t=4))
        vec_bank = new_bank("vec")
        for t in range(4):
            nc.tensor.transpose(vec_bank[:, P * t : P * (t + 1)], vec_f32[:, t, :], ident[:])
        nc.scalar.copy(out=vec_cols[:], in_=vec_bank[:].rearrange("p (t v) -> p t v", t=4)[:, :, 0:36])
        permute_p(0, 0, 2)
        permute_p_plane(0, 0, 2)
        warm = new_bank("warm")
        for i in range(3):
            nc.tensor.matmul_mx(
                out=warm[:],
                lhsT=p_codes[:, 0, 0, :].bitcast(FP4X4),
                lhsT_scale=p_plane[:, 0, 0, :],
                rhs=p_codes[:, 0, :, :].rearrange("p k c -> p (k c)").bitcast(FP4X4),
                rhs_scale=p_plane[:, 0, :, :].rearrange("p k c -> p (k c)"),
                start=True,
                stop=True,
            )
        permute_p(0, 2, 4)
        permute_p_plane(0, 2, 4)
        permute_p_plane(1, 0, 4)
        nc.vector.tensor_tensor(
            out=lam_floored[:], in0=vec_cols[:, :, 32:34], in1=vec_cols[:, :, 34:36], op=ALU.max
        )
        nc.vector.tensor_tensor(out=gain[:], in0=vec_cols[:, :, 0:4], in1=vec_cols[:, :, 4:8], op=ALU.mult)
        nc.vector.tensor_scalar(
            out=neg_mu[:], in0=vec_cols[:, :, 8:12], scalar1=-1.0, scalar2=None, op0=ALU.mult
        )

        def z_narrow(half, on_vector=()):
            for pair in range(2):
                bank = new_bank(("zn", half, pair))
                for s in range(2):
                    stage1(bank[:, 256 * s : 256 * (s + 1)], half, 2 * pair + s, NARROW)
                for s in range(2):
                    evac_h(bank[:, 256 * s : 256 * (s + 1)], half, 2 * pair + s, NARROW, 2 * pair + s not in on_vector)

        def z_wide(half, t):
            stage1(new_bank(("z", half, t))[:], half, t, WIDE)
            evac_h(banks[("z", half, t)][:], half, t, WIDE)

        def g_narrow(g, on_vector=()):
            y_t[(g, 512)] = ring.tile([P, 4, 256], F32, name="y_t_narrow", bufs=3, align_bytes=64)
            for pair in range(2):
                bank = new_bank(("gn", g, pair))
                for s in range(2):
                    stage2(bank[:, 256 * s : 256 * (s + 1)], g, 2 * pair + s, NARROW)
                for s in range(2):
                    evac_y(bank[:, 256 * s : 256 * (s + 1)], g, 2 * pair + s, NARROW, 2 * pair + s not in on_vector)

        def g_wide(g, on_vector=()):
            y_t[(g, 0)] = ring.tile([P, 4, 512], F32, name="y_t_wide", bufs=3, align_bytes=64)
            for t in range(4):
                stage2(new_bank(("g", g, t))[:], g, t, WIDE)
                evac_y(banks[("g", g, t)][:], g, t, WIDE, t not in on_vector)

        def turn(g, j, on_scalar=True):
            if j % 2 == 0:
                y_rows[(g, j)] = ring.tile([P, 2, 512], F32, name="y_rows", bufs=6, align_bytes=64)
            turn_y(g, j)
            evac_turned(g, j, on_scalar)
            if j % 2 == 1:
                store_y(g, j - 1, j + 1)

        def vt_unit(g, half, s0=False):
            group_vt(g, half, on_scalar=s0, part=0)
            group_vt(g, half, part=1)

        def y_planes(g, cols):
            group_y(g, cols)
            quantize_y(g, cols)
            store_codes(g, cols)

        z_wide(0, 0)
        group_vt(0, 0)
        permute_p(1, 0, 4)
        z_wide(0, 1)
        vt_unit(1, 0, True)
        quantize_vt(0, 0)
        z_wide(0, 2)
        z_wide(0, 3)
        quantize_vt(1, 0)
        group_h(0, WIDE)
        z_wide(1, 0)
        z_wide(1, 1)
        group_vt(0, 1)
        quantize_h(0, WIDE)
        vt_unit(1, 1, True)
        quantize_vt(0, 1)
        z_wide(1, 2)
        z_wide(1, 3)
        group_h(1, WIDE)
        quantize_vt(1, 1)
        quantize_h(1, WIDE)
        group_vt(3, 0, on_scalar=True, part=0)
        z_narrow(0)
        group_vt(2, 0, on_scalar=True, part=0)
        group_vt(3, 0, part=1)
        group_h(0, NARROW)
        z_narrow(1)
        group_h(1, NARROW)
        quantize_h(0, NARROW)
        quantize_h(1, NARROW)
        g_wide(0)
        g_narrow(0)
        group_vt(2, 0, part=1)
        group_vt(2, 1)
        group_y(0, WIDE)
        group_y(0, NARROW)
        for j in range(6):
            turn(0, j, j not in (2, 4))
            if j == 2:
                quantize_y(0, WIDE)
                quantize_y(0, NARROW)
                store_codes(0, slice(0, B))
        quantize_vt(2, 0)
        quantize_vt(2, 1)
        g_wide(1)
        g_narrow(1)
        group_y(1, WIDE)
        for j in range(6):
            turn(1, j, j not in (2, 4))
            if j == 2:
                group_y(1, NARROW)
        quantize_y(1, WIDE)
        quantize_y(1, NARROW)
        store_codes(1, slice(0, B))
        group_vt(3, 1)
        quantize_vt(3, 0)
        quantize_vt(3, 1)
        g_wide(2)
        g_narrow(2)
        for j in range(6):
            turn(2, j, j not in (2, 4))
            if j == 2:
                group_y(2, NARROW)
        group_y(2, WIDE)
        quantize_y(2, NARROW)
        quantize_y(2, WIDE)
        store_codes(2, slice(0, B))
        store_scales(0, 3)
        g_wide(3)
        g_narrow(3)
        group_y(3, WIDE)
        for j in range(6):
            turn(3, j, j not in (1,))
            if j == 1:
                group_y(3, NARROW)
                quantize_y(3, WIDE)
                quantize_y(3, NARROW)
        store_codes(3, slice(0, B))
        store_scales(3, 4)
